import numpy as np, ml_dtypes
CORES = [2,3,42,43,82,83,122,123]
N = 8
import mx_ref
BF = ml_dtypes.bfloat16
def gentries(a):
    return np.ascontiguousarray(a.reshape(8, 16, -1).transpose(0, 2, 1)).reshape(8, -1)
def gtable(e):
    e = np.asarray(e); return np.ascontiguousarray(e.reshape(8, -1, 16).transpose(0, 2, 1)).reshape(128, -1).astype(np.int32)
def gcols(t, e):
    v = np.concatenate([t.reshape(8, 16, -1, 4), np.zeros((8, 16, 1, 4), BF)], axis=2)
    return np.ascontiguousarray(np.stack([v[g][:, e[g]] for g in range(8)])).reshape(128, -1)
def tile(rs):
    return np.stack(rs, axis=2).reshape(128, -1).astype(BF)
def pick(q, e):
    c = np.concatenate([q[0].reshape(128, -1, 4), np.zeros((128, 1, 4), np.uint8)], axis=1); s = np.concatenate([q[1], np.ones((16, 1), np.uint8)], axis=1)
    return (np.ascontiguousarray(c[:, e].reshape(128, -1)), np.ascontiguousarray(s[:, e]))
def join(*qs):
    return (np.concatenate([q[0] for q in qs], axis=1), np.concatenate([q[1] for q in qs], axis=1))
def put(q, e, v):
    c, s = q[0].reshape(128, -1, 4).copy(), q[1].copy(); c[:, e] = v[0].reshape(128, -1, 4); s[:, e] = v[1]
    return (c.reshape(128, -1), s)
def pk(c, s):
    return (np.ascontiguousarray(c), mx_ref.live(s))
def emit(q):
    return q[0], q[1]
def packed(v, rng):
    q = [mx_ref.quantize(np.ascontiguousarray(v[r])) for r in range(N)]
    return np.stack([a for a, b in q]), np.stack([mx_ref.plane(b, rng) for a, b in q])
def values_of_codes():
    e, c = np.zeros((128, 128, 4), np.float32), np.zeros((128, 2, 4), np.uint8)
    e[np.arange(128), np.arange(128), 0] = 1
    c[:127, :, 0] = np.arange(256).reshape(2, 128).T[:127]
    return mx_ref.matmul(mx_ref.quantize(e.reshape(128, 512).astype(BF)), (c.reshape(128, 8), np.full((16, 2), 127, np.uint8))).T.reshape(-1).astype(np.float64)
CODE_VALUE, SCALE_VALUE = values_of_codes(), 2.0 ** (np.arange(256) - 127.0)
def decode(q):
    return (CODE_VALUE[q[0]].reshape(16, 8, -1, 4) * SCALE_VALUE[q[1]][:, None, :, None] + 0.0).reshape(128, -1).astype(np.float32)
def f(rng, *shape):
    return mx_ref.flush((rng.standard_normal(shape, dtype=np.float32) * np.exp2(rng.integers(-2, 3, shape[:-1] + (1,)))).astype(BF))
def wide(rng, *shape, cols=0):
    v = rng.standard_normal(shape, dtype=np.float32) * np.exp2(rng.integers(-12, 13, shape)).astype(np.float32)
    if cols: v *= np.repeat(np.exp2(rng.integers(-cols, cols + 1, shape[:-2] + (1, shape[-1] // 4))) * (rng.random(shape[:-2] + (1, shape[-1] // 4)) > 0.0625), 4, axis=-1).astype(np.float32)
    return mx_ref.flush(v.astype(BF))
C, T, R = 256, 2048, 3
def big(v):
    v = v.astype(np.float32)
    v[np.abs(v) < np.float32(2.0 ** -12)] = 0
    return v.astype(BF)
def numbers_of(rng):
    return {"x": big(f(rng, N, 128, 4 * C)), "u": np.array(f(rng, N, 128, 512)), "v": np.array(f(rng, N, 128, 512))}
def lists_of(t):
    return np.stack([gtable(t[r]) for r in range(N)])
def layers(rng, still=[], full=False):
    w = np.zeros((N, 512, 512), np.float32)
    k = rng.random((N, 512, 512))
    k[:, :, np.isin(np.arange(512) // 4 % 16, still)] = 2
    e = np.argpartition(k, 8, axis=2)[:, :, :8]
    a = rng.integers(4, 16, (N, 512, 8)) * 0.25 * rng.choice([-1.0, 1.0], (N, 512, 8))
    if full: a = 4.0 * rng.choice([-1.0, 1.0], (N, 512, 1)) * np.ones((1, 1, 8))
    np.put_along_axis(w, e, a.astype(np.float32), axis=2)
    w[:, np.isin(np.arange(512) % 16, still)] = 0
    return w
def weights(rng, w):
    c, s = packed(np.ascontiguousarray(w.reshape(N, 512, 128, 4).transpose(0, 2, 1, 3)).reshape(N, 128, 2048).astype(BF), rng)
    return {"wc": c, "ws": s}
def setup_inputs(rng):
    return {**numbers_of(rng), "p": lists_of(rng.integers(0, T, (N, 8, C))), **weights(rng, layers(rng))}
def setup_inputs_ties(rng):
    d = numbers_of(rng)
    x = d["x"].reshape(N, 8, 16, C, 4)
    x[:, :, 0] = 0
    x[:, :, 0, :, 0] = rng.integers(0, 3, (N, 8, C)).astype(np.float32).astype(BF)
    u = d["u"].reshape(N, 128, 128, 4)
    u[:, :, ::16] = 0
    o = rng.permutation(N)
    for r in range(N):
        for h in range(0, 128, 16): u[r, h, h, 0] = 0.0 if r == o[0] else -1.0 if r == o[1] else 1.0
    t = rng.integers(0, T, (N, 8, C))
    t[o[:2]] = C * rng.integers(0, 4, (2, 8, C))
    t[o[2]] = rng.integers(0, T)
    t[o[3]] = C * (7 - np.arange(8))[:, None]
    return {"x": x.reshape(N, 128, 4 * C), "u": u.reshape(N, 128, 512), "v": d["v"], "p": lists_of(t), **weights(rng, layers(rng, [0]))}
def setup_inputs_near(rng):
    d = numbers_of(rng)
    x = d["x"].astype(np.float32).reshape(N, 8, 16, C, 4)
    x[:, :, 0] = 0
    x[:, :, 8:] = 0
    u = d["u"].reshape(N, 128, 128, 4)
    u[:, :, ::16] = 0
    t = rng.integers(0, T, (N, 8, C))
    o = rng.permutation(N) % 4
    for r in range(N):
        s = rng.integers(0, 16, (8, C))
        if o[r] == 1:
            s[5:] = np.minimum(s[5:], 12)
            s[5:, 4:9] = [15, 15, 14, 13, 12]
            t[r] = np.minimum(t[r], T - 2)
            t[r, 5, :16] = T - 1
            t[r, 6, :9] = T - 1
            t[r, 7, :7] = T - 1
        if o[r] < 3: x[r, :, 8] = ((s[:, :, None] >> np.arange(4)) & 1) * np.exp2(np.arange(4) - 22.0)
        if o[r] < 2:
            x[r, :, 0, :, 0] = rng.choice([-1.0, 1.0], (8, 1))
            x[r, :, 11, :, 0] = 2.0 ** -10
        if o[r] == 2:
            for g in rng.permutation(8)[:4]: x[r, g, 0, rng.integers(C), 0] = 2.0 ** 26 * rng.choice([-1.0, 1.0])
        if o[r] == 3:
            x[r, :, 10, :, 0] = np.where(s < 8, 1.125 * 2.0 ** -29, 0.0)
            x[r, :, 11, :, 0] = np.where(s < 8, 0.0, 2.0 ** -29)
        k = 1.0 if o[r] == 0 else 2.0 ** -30
        for h in range(0, 128, 16):
            if o[r] < 2:
                u[r, h, h, 0] = k
                u[r, h + 11, h, 0] = k
            if o[r] == 2: u[r, h, h, 0] = 2.0 ** 30
            if o[r] < 3: u[r, h + 8, h] = k
            else:
                u[r, h + 10, h, 0] = 1.125 * k
                u[r, h + 11, h, 0] = 1.25 * k
    return {"x": x.reshape(N, 128, 4 * C).astype(BF), "u": u.reshape(N, 128, 512), "v": d["v"], "p": lists_of(t), **weights(rng, layers(rng, [0, 8, 9, 10, 11, 12, 13, 14, 15]))}
def setup_inputs_fine(rng):
    d = numbers_of(rng)
    x = (1.0 + (2 * rng.integers(0, 64, (N, 8, 2, 8, C, 4)) + 1) * 2.0 ** -7) * np.exp2(-rng.integers(8, 15, (N, 8, 2, 8, C, 4))) * rng.choice([-1.0, 1.0], (N, 8, 2, 8, C, 4))
    np.put_along_axis(x[..., 0], rng.integers(0, 8, (N, 8, 2, 1, C)), 1.96875 * rng.choice([-1.0, 1.0], (N, 8, 2, 1, C)), axis=3)
    x = x * np.exp2(rng.integers(-1, 3, (N, 8, 2, 1, C, 1)))
    return {"x": x.astype(np.float32).reshape(N, 128, 4 * C).astype(BF), "u": d["u"], "v": d["v"], "p": lists_of(rng.integers(0, T, (N, 8, C))), **weights(rng, layers(rng))}
def setup_inputs_ends(rng):
    k = int(rng.integers(0, 2))
    o = np.roll(np.array([2, 3, k, 1 - k])[np.arange(N) % 4], int(rng.integers(0, N)))
    sign = np.array([1.0, -1.0, 1.0, 1.0])
    x = np.zeros((N, 8, 16, C, 4))
    u = np.array(f(rng, N, 128, 512)).reshape(N, 128, 128, 4)
    v = (rng.integers(0, 2, (N, 128, 512)) * 2.0 - 1.0) * 2.0 ** 30
    w = layers(rng, full=True)
    t = np.zeros((N, 8, C), np.int64)
    for r in range(N):
        a = 2.0 ** 26 * rng.choice([1.0, 0.875, 0.75], (8, 1, C, 1))
        if o[r] == 0: x[r] = a
        if o[r] == 1:
            x[r] = -a
            t[r] = T - 1
        if o[r] < 2:
            w[r] = np.abs(w[r]) * (sign[o[r]] * sign[o[r - 1]])
            if o[r - 1] == 3:
                w[r, :, :64] = np.sum(w[r].reshape(512, 8, 64), axis=1)
                w[r, :, 64:] = 0
        if o[r] == 2:
            x[r] = 2.0 ** -30
            w[r] = 0
            t[r] = (T - 1) * rng.integers(0, 2, (8, C))
        if o[r] == 3:
            x[r] = 2.0 ** 26 * rng.choice([-1.0, 1.0], (8, 1, C, 1))
            x[r, 0] = 2.0 ** 26
            t[r] = (T - 1) * (rng.permutation(8) % 2)[:, None]
        h = rng.permutation(6) % 2 * 2.0 - 1.0
        for g in range(8): u[r, :, 16 * g] = 0.0 if g in (0, 7) else (2.0 ** -30 if o[r] == 2 else 2.0 ** 30) * float(h[g - 1])
    v = (np.where(v < 0, -1.0, 1.0) * np.where(rng.permutation(N) % 2, 2.0 ** -30, 2.0 ** 30)[:, None, None]).astype(np.float32).astype(BF)
    return {"x": x.astype(np.float32).reshape(N, 128, 4 * C).astype(BF), "u": u.reshape(N, 128, 512), "v": v.astype(np.float32).astype(BF), "p": lists_of(t), **weights(rng, w)}
def setup_inputs_spread(rng):
    d = setup_inputs(rng)
    d["x"] = big(wide(rng, N, 128, 4 * C, cols=6))
    return d
def check_inputs(d):
    b = []
    for k, most in (("x", 2.0 ** 26), ("u", 2.0 ** 30), ("v", 2.0 ** 30)):
        a = np.abs(d[k].astype(np.float32))
        if not (np.isfinite(a).all() and ((a == 0) | (a >= 2.0 ** -30) & (a <= most)).all()): b.append("a value of " + k)
    if not ((d["p"] >= 0) & (d["p"] < T)).all(): b.append("an entry of p")
    none, least, most = [emit(mx_ref.quantize(np.full((128, 16), k, np.float32).astype(BF)))[1][0, 0] for k in (0.0, 2.0 ** -30, 2.0 ** 30)]
    for r in range(N):
        if ((d["wc"][r] == 0x7F) | (d["wc"][r] == 0xFF)).any(): b.append("wc: a code that is no number")
        s = mx_ref.live(d["ws"][r])
        if ((s != none) & ((s < least) | (s > most))).any(): b.append("ws: a scale out of range")
        a = np.abs(decode(pk(d["wc"][r], d["ws"][r])).astype(np.float64)).reshape(128, 512, 4)
        if not (np.sum(a, axis=(0, 2)) <= 32).all(): b.append("sizes in a column of W")
    return b
def order_of(t):
    place = np.argsort(np.argsort(T * t.reshape(-1) + np.arange(T))).reshape(8, C)
    o = np.argsort(place, axis=1)
    k = np.stack([np.searchsorted(place[g, o[g]], 8 * np.arange(C) + 7, side="right") for g in range(8)]) - 1
    k = np.maximum(k, 0)
    return place // 8, np.take_along_axis(o, k, axis=1), np.take_along_axis(o, np.minimum(k + 1, C - 1), axis=1)
def reference(x, u, v, p, wc, ws):
    qu = [mx_ref.quantize(u[r]) for r in range(N)]
    lay = [pk(wc[r], ws[r]) for r in range(N)]
    now = [x[r] for r in range(N)]
    pos = np.stack([gentries(p[r]) for r in range(N)]).astype(np.int64)
    for t in range(R):
        own, q = [], []
        for r in range(N):
            own.append(decode(mx_ref.quantize(now[r])).astype(BF))
            c, m, n = order_of(pos[r])
            z = ((gcols(own[r], m).astype(np.float32) + gcols(own[r], n).astype(np.float32)) * np.float32(0.5)).astype(BF)
            q.append(mx_ref.quantize(z))
            s = mx_ref.matmul(qu[r], q[r])[::16] + np.float32(0.0)
            step = np.argsort(np.argsort(s, axis=1, kind="stable"), axis=1)
            pos[r] += np.take_along_axis(step, c, axis=1)
        for r in range(N):
            came = pick(q[(r + N - 1) % N], np.arange(1, C, 2))
            h = tile([mx_ref.matmul(pick(lay[r], np.arange(128 * b, 128 * b + 128)), came) * np.float32(0.03125) for b in range(4)])
            c, m, n = order_of(pos[r])
            now[r] = (own[r].astype(np.float32) + gcols(h, c // 2).astype(np.float32)).astype(BF)
    y, pt = np.zeros((N, 128, C), np.float32), np.zeros((N, 8, C), np.float32)
    oc, osc = np.zeros((N, 128, 4 * C), np.uint8), np.zeros((N, 16, C), np.uint8)
    for r in range(N):
        q = mx_ref.quantize(now[r])
        y[r] = mx_ref.matmul(mx_ref.quantize(v[r]), q)
        pt[r] = pos[r]
        oc[r], osc[r] = emit(q)
    return {"y": y, "pt": pt, "oc": oc, "osc": osc}

from concourse.mybir import dt, AluOpType as A, ActivationFunctionType as AF

N, R, C = 8, 3, 256
TW = 2816
HW = 2824
ZI = 2816
NV = 7
NS = 7
F8 = "float8_e4m3fn_x4"
LISTS = {}


def _scratch():
    s = {}

    def sb(names, w, d="float32"):
        for n in names.split(): s[n] = ("sbuf", [128, w], d)

    def mx(n, m, w):
        sb(n, w, F8)
        sb(m, w, "uint8")

    def lists(buf, d, names, wide):
        at = 0
        for n in names.split():
            w = wide.get(n, 16)
            LISTS[n] = (buf, at, w)
            at += (w + 15) // 16 * 16
        sb(buf, at, d)
    lists("lstf", "float32", "kl el elf Dm De t16 Kl acc rl lo eqv dm of eqc dmc ofc ivl cf cp kl17 pls lk par", {"kl17": 17, "pls": 17, "lk": 32, "par": 4})
    lists("lsti", "int32", "iB pl sh4 colI c_lo c_hi place sh3 tt ip iq", {"place": 17, "sh3": 17, "tt": 32, "ip": 2, "iq": 2})
    lists("lstu", "uint16", "kapU rep oddl ul ru ou lou oc2 hu cu ku colU piU iu x40 x41 x42 x43 L2", {"L2": 34})
    sb("iA iX amod prow pti", 256, "int32")
    sb("mask m0 er V Krow k2 Ko mk2 sl SBt dd crow stw inv prs ior ptf yo keepf", 256)
    sb("ks", 264)
    sb("mkb mko keepb kval kvale mg mgo Wr kpw", 256, "bfloat16")
    sb("junk", 256 * (16 - NV), "bfloat16")
    sb("sgn", 256 * NS, "bfloat16")
    sb("cmp", 256 * NV, "bfloat16")
    sb("sc", 128 * NV + 128, "float16")
    sb("sc2", 288)
    sb("h", HW + 256, "bfloat16")
    sb("tabs", HW, "bfloat16")
    sb("tab2", TW + 16, "bfloat16")
    sb("gt gtT", 544, "bfloat16")
    sb("Wc uin vin Bt0 Bt Bh Bm H", 512, "bfloat16")
    sb("Ct", 4096, "bfloat16")
    sb("Dt Z P F G XP Xf xin", 1024, "bfloat16")
    sb("X", 1088, "bfloat16")
    sb("EE one", 520, "bfloat16")
    for t in range(4): mx("ec%d" % t, "es%d" % t, 128)
    for n, m, w in (("bc", "bs", 128), ("hc", "hs", 128), ("mc", "ms", 128), ("xq", "xs", 272), ("zq", "zs", 256), ("cq", "cs", 1024), ("dq", "dqs", 256),
                    ("uq", "us", 128), ("u2", "u2s", 128), ("vq", "vqs", 128), ("wq", "wp", 512), ("fq", "fqs", 256)): mx(n, m, w)
    for k in range(R):
        mx("pk%d" % k, "pp%d" % k, 128)
        mx("lc%d" % k, "lp%d" % k, 128)
    for k in range(8): s["ps%d" % k] = ("psum", [128, 512], "float32")
    return s


SCRATCH = _scratch()
DSEM = ["dp", "drow", "dx", "du", "dw", "dv", "div", "dend"] + [n + str(k) for n in ("dV", "dlk", "dlo", "dk2", "dtab") for k in range(R + 1)]
SEMAPHORES = ["qV", "qS", "qT", "qG", "snd"] + ["arr%d" % k for k in range(R)] + DSEM


def rank_program(g, core, T, topo):
    rank = T.rank_of(core)
    if rank is None:
        return
    eng = {"V": g.vector, "S": g.scalar, "T": g.tensor, "G": g, "Y": g.sync}
    know = {q: {} for q in eng}
    cnt, last, readers, ends = {}, {}, {}, {}

    def c(name, a=0, b=None, step=1):
        buf, at, w = LISTS[name]
        return T[buf][:, at + a:at + (w if b is None else b):step]

    def need(q, toks):
        best = {}
        for t in toks:
            if t[1] > best.get(t[0], (0, 0))[1]: best[t[0]] = t
        for t in sorted(best.values(), key=lambda t: -len(t[3])):
            if know[q].get(t[0], 0) >= t[1]: continue
            eng[q].wait_ge(T.sem[t[0]], t[1])
            for s, v in t[3].items():
                if v > know[q].get(s, 0): know[q][s] = v
            know[q][t[0]] = t[1]

    def deps(q, rd, wr, acc=False, copies=False):
        d = []
        for k in rd:
            if k in last: d.append(last[k])
            if k[:2] == "ps": d += [t for t in readers.get(k, []) if t[2] != q]
        for k in wr:
            if k in last and not (acc and last[k][2] == q): d.append(last[k])
            d += [t for t in readers.get(k, []) if copies or t[2] != q]
        return d

    def note(tok, rd, wr):
        for k in rd: readers.setdefault(k, []).append(tok)
        for k in wr:
            last[k] = tok
            readers[k] = []

    def op(q, rd, wr, fn, *a, acc=False, **kw):
        need(q, deps(q, rd, wr, acc))
        s = "q" + q
        cnt[s] = cnt.get(s, 0) + 1
        fn(*a, **kw).then_inc(T.sem[s], 1)
        note((s, cnt[s], q, {**know[q], s: cnt[s]}), rd, wr)
        ends[s] = cnt[s]

    def dma(sem, items):
        seen, rds, wrs = {}, [], []
        for q, o, i, rd, wr in items: need(q, deps(q, rd, wr, copies=True))
        for q, o, i, rd, wr in items:
            cnt[sem] = cnt.get(sem, 0) + 16
            eng[q].dma_start(o, i).then_inc(T.sem[sem], 16)
            for s, v in know[q].items(): seen[s] = max(v, seen.get(s, 0))
            rds += rd
            wrs += wr
        seen[sem] = cnt[sem]
        note((sem, cnt[sem], "dma", seen), rds, wrs)
        ends[sem] = cnt[sem]

    V, S, PE = g.vector, g.scalar, g.tensor
    vts, vtt, vcp, vscan, act = V.tensor_scalar, V.tensor_tensor, V.tensor_copy, V.tensor_tensor_scan, S.activation

    def quant(qn, sn, tn, a, n):
        op("V", [tn], [qn, sn], V.quantize_mx, T[qn][:, 0:n], T[sn][:, 0:n], T[tn][:, a:a + 4 * n])

    def mm(bank, lq, ls, la, rq, rs, ra, n, start=True, stop=True):
        op("T", [lq, ls, rq, rs], [bank], PE.matmul_mx, T[bank][:, 0:n], T[lq][:, la:la + 128], T[ls][:, la:la + 128],
           T[rq][:, ra:ra + n], T[rs][:, ra:ra + n], start, stop, acc=not start)

    dma("dp", [("Y", c("pl"), T.p[:], [], ["pl"])])
    dma("drow", [("YS"[x % 2], T.prow[x::16, :], T.p[:], [], ["prow"]) for x in range(16)])
    dma("dx", [("Y", T.xin[:], T.x[:], [], ["xin"])])
    dma("du", [("S", T.uin[:], T.u[:], [], ["uin"])])

    def iota(n, pat, base=0, cm=0, small=False):
        out = c(n) if n in LISTS else T[n][:]
        if small: op("G", [], [n], g.iota, out, pat, base, cm, allow_small_or_imprecise_dtypes=True)
        else: op("G", [], [n], g.iota, out, pat, base, cm)

    def zeros(n, w, after=()):
        op("G", list(after), [n], g.iota, T[n][:], [[0, w]], 0, 0, allow_small_or_imprecise_dtypes=True)
    iota("iB", [[1, 16]])
    iota("iA", [[0, 256]], 0, 1)
    iota("er", [[1, 256]], small=True)
    iota("iX", [[0, 16], [1, 16]])
    iota("V", [[1, 256]], small=True)
    iota("kval", [[1, 16], [16, 16]], 1, small=True)
    iota("ip", [[0, 2]], 0, 1)
    op("V", ["iA"], ["amod"], vts, T.amod[:], T.iA[:], 15, None, A.bitwise_and)
    a16 = T.amod[:, 0:16]
    op("V", ["iB"], ["of"], vts, c("of"), c("iB"), 16.0, None, A.mult)
    op("V", ["amod"], ["t16"], vts, c("t16"), a16, 16.0, None, A.mult)
    op("V", ["of", "amod"], ["el"], vtt, c("el"), c("of"), a16, A.add)
    op("V", ["t16", "iB"], ["kl"], vtt, c("kl"), c("t16"), c("iB"), A.add)
    op("S", ["er"], ["er"], act, T.er[:], T.er[:], AF.Copy, scale=1.0 / 256)
    op("V", ["el"], ["elf"], vts, c("elf"), c("el"), 1.0 / 256, None, A.mult)
    op("V", ["kl"], ["kapU"], vcp, c("kapU"), c("kl"))
    op("V", [], ["one"], V.memset, T.one[:], 0.5)
    op("V", [], ["Bt0"], V.memset, T.Bt0[:], 1.0)
    op("V", [], ["ks"], V.memset, T.ks[:, 256:264], TW - 1.0)
    op("V", [], ["sc"], V.memset, T.sc[:, 0:128], 0.0)
    op("V", ["amod", "iX"], ["mask"], vtt, T.mask[:], T.amod[:], T.iX[:], A.is_equal)
    op("V", ["iX"], ["keepf"], vts, T.keepf[:], T.iX[:], 1.0, None, A.min)
    op("V", ["iX"], ["keepb"], vts, T.keepb[:], T.iX[:], 1.0, None, A.min)
    op("V", ["pl", "elf"], ["Kl"], vtt, c("Kl"), c("pl"), c("elf"), A.add)
    op("V", ["prow", "kapU", "er"], ["Krow"], vtt, T.Krow[:], T.prow[:].indirect(c("kapU")), T.er[:], A.add)
    op("G", ["one"], ["EE"], g.affine_select, T.EE[:], T.one[:], [[-1, 520]], A.is_equal, 0.0, 4, 4)
    zeros("tab2", TW + 16)
    op("G", ["Bt0"], ["Bt"], g.affine_select, T.Bt[:], T.Bt0[:], [[-16, 8], [0, 64]], A.is_ge, 0.0, 0, 1)
    op("G", ["Bt"], ["Bt"], g.affine_select, T.Bt[:], T.Bt[:], [[16, 8], [0, 64]], A.is_ge, 0.0, 15, -1)
    iota("kvale", [[1, 256]], 1, small=True)
    zeros("Wc", 512)
    zeros("Ct", 4096)
    zeros("Dt", 1024)

    def consts1():
        op("V", [], ["h"], V.memset, T.h[:], 0.0)
        op("V", ["kl"], ["Dm"], vts, c("Dm"), c("kl"), HW - 1.0, None, A.add)
        op("V", ["ip"], ["iq"], vts, c("iq"), c("ip"), 4, 1, A.arith_shift_right, A.bitwise_and)
        op("V", ["iq"], ["par"], vcp, c("par", 0, 1), c("iq", 0, 1))
        op("V", ["par"], ["par"], vts, c("par", 1, 2), c("par", 0, 1), -1.0, 1.0, A.mult, A.add)
        op("V", ["par"], ["par"], vts, c("par", 2, 4), c("par", 0, 2), float(ZI), None, A.mult)
        for t in range(4): quant("ec%d" % t, "es%d" % t, "EE", 4 - t, 128)

    def consts2():
        op("V", ["kl"], ["kl17"], vcp, c("kl17", 0, 16), c("kl"))
        op("V", ["kl"], ["kl17"], vts, c("kl17", 16, 17), c("kl", 15, 16), 1.0, None, A.add, acc=True)
        op("V", [], ["sc2"], V.memset, T.sc2[:, 0:16], 0.0)
        op("V", ["el"], ["De"], vts, c("De"), c("el"), 256.0, None, A.add)
        op("S", ["Bt"], ["Bh"], act, T.Bh[:], T.Bt[:], AF.Copy, scale=0.5)
        for t in range(4): op("S", ["Bt"], ["Bm"], act, T.Bm[:, t::4], T.Bt[:, t::4], AF.Copy, scale=1.0 if 8 + t < 16 - NS else 0.5, acc=t > 0)
        op("V", ["iB"], ["ul"], vts, c("ul"), c("iB"), 16.0, None, A.mult)
        op("V", ["iB"], ["rep"], vts, c("rep"), c("iB"), 16.0, 15.0, A.mult, A.add)
        op("V", ["el"], ["oddl"], vts, c("oddl"), c("el"), 2.0, 1.0, A.mult, A.add)
        quant("uq", "us", "uin", 0, 128)
        op("V", [], ["crow"], V.memset, T.crow[:, 0:256 - 16 * NS], 8.0 * NS)
        op("V", ["uq", "ul"], ["u2"], vcp, T.u2[:].bitcast(dt.uint32), T.uq[:].bitcast(dt.uint32).indirect(c("ul", 0, 8)))
        op("V", ["us", "ul"], ["u2s"], vcp, T.u2s[:], T.us[:].indirect(c("ul", 0, 8)))
        op("V", [], ["crow"], V.memset, T.crow[:, 256 - 16 * NS:256], 8.0 * NS - 8, acc=True)
        op("V", ["amod", "iX"], ["m0"], vtt, T.m0[:], T.amod[:], T.iX[:], A.is_lt)
        quant("bc", "bs", "Bt", 0, 128)
        op("V", ["m0"], ["m0"], vts, T.m0[:], T.m0[:], -1e-35, None, A.mult)

    def order_begin(n):
        dma("dV%d" % n, [("Y", T.V[0::2, :], T.Krow[0::2, :], ["Krow"], ["V"])])
        for b in range(NV, 16):
            op("S", ["Krow", "Kl"], ["junk", "acc"], act, T.junk[:, 256 * (b - NV):256 * (b - NV) + 256], T.Krow[:], AF.Sign, bias=c("Kl", b, b + 1), scale=-1.0,
               accum_out=c("acc", b, b + 1), acc=b > NV)
        for b in range(NV):
            op("V", ["Krow", "Kl"], ["cmp"], vts, T.cmp[:, 256 * b:256 * b + 256], T.Krow[:], c("Kl", b, b + 1), None, A.is_lt, acc=True)
        w = 128 * NV
        op("V", ["cmp"], ["sc"], vscan, T.sc[:, 128:128 + w], T.cmp[:, 0:2 * w:2], T.cmp[:, 1:2 * w:2], 0.0, A.add, A.add)
        op("V", ["acc"], ["ruS"], vts, c("ru", NV, 16), c("acc", NV, 16), 0.5, 127.5, A.mult, A.add)
        op("V", ["sc"], ["rl"], vtt, c("rl", 0, NV), T.sc[:, 255::128], T.sc[:, 127:127 + w:128], A.subtract)
        op("V", ["rl"], ["ruV"], vcp, c("ru", 0, NV), c("rl", 0, NV))
        op("V", ["ruS", "ruV", "V"], ["ks"], vcp, T.ks[:, 0:256].indirect(c("ru")), T.V[:])
        dma("dlk%d" % n, [("Y", c("lk", 0, 16), T.ks[0::16, 0:256], ["ks"], ["lk"]), ("Y", c("lk", 16, 32), T.ks[0::16, 1:257], ["ks"], ["lk"])])
        dma("dlo%d" % n, [("Y", c("lo"), T.ks[1::16, 0:256], ["ks"], ["lo"])])
        dma("dk2%d" % n, [("Y", T.k2[0::2, :], T.ks[0::2, 0:256], ["ks"], ["k2"]), ("Y", T.k2[1::2, :], T.ks[0::2, 0:256], ["ks"], ["k2"])])

    def order_tables(n):
        t0, t1 = c("tt", 0, 16), c("tt", 31, 32)
        op("V", ["lk"], ["tt"], vts, c("tt"), c("lk"), -0.498, None, A.add)
        op("V", ["tt"], ["eqv"], vtt, c("eqv"), t0, c("tt", 16, 32), A.is_equal)
        op("V", ["eqv", "Dm"], ["dm"], vtt, c("dm"), c("eqv"), c("Dm"), A.mult)
        op("V", ["tt", "dm"], ["of"], vtt, c("of"), c("dm"), t0, A.max)
        op("V", ["of"], ["ou"], vts, c("ou"), c("of"), 1.0, None, A.add)
        op("V", ["ou", "kval"], ["h"], vcp, T.h[:].indirect(c("ou")), T.kval[:])
        op("V", ["h"], ["tabs"], vscan, T.tabs[:], T.h[:, 0:HW], T.h[:, 0:HW], 0.0, A.max, A.max)
        items = []
        for e in range(N):
            if e < N - 1: items.append((T.tab2[17 * e + 16::16, 0:TW], T.tabs[16 * e:16 * e + 7 - e, 1:TW + 1]))
            if e: items.append((T.tab2[e:16 * e:16, 0:TW], T.tabs[16 * e:16 * e + e, 0:TW]))
        dma("dtab%d" % n, [("YS"[k % 2], o, i, ["tabs"], ["tab2"]) for k, (o, i) in enumerate(items)])
        op("V", ["tt", "par"], ["L2a"], vts, c("L2", 0, 32, 2), t0, c("par", 1, 2), c("par", 2, 3), A.mult, A.add)
        op("V", ["tt", "par"], ["L2b"], vts, c("L2", 1, 32, 2), t0, c("par", 0, 1), c("par", 3, 4), A.mult, A.add)
        op("V", ["tt", "par"], ["L2c"], vts, c("L2", 32, 33), t1, c("par", 1, 2), c("par", 2, 3), A.mult, A.add)
        op("V", ["tt", "par"], ["L2d"], vts, c("L2", 33, 34), t1, c("par", 0, 1), c("par", 3, 4), A.mult, A.add)
        if n < R: zeros("h", HW + 256, ["tabs"])

    def order_places():
        op("V", ["tab2", "L2a", "L2b", "L2c", "L2d"], ["gt"], vcp, T.gt[:], T.tab2[:].indirect(c("L2")))
        op("V", ["gt"], ["gtT"], V.transpose, T.gtT[:], T.gt[:])
        op("V", ["gtT"], ["sc2"], vscan, T.sc2[:, 16:288], T.gtT[:, 0::2], T.gtT[:, 1::2], 0.0, A.add, A.add)
        op("V", ["sc2"], ["pls"], vtt, c("pls"), T.sc2[:, 31::16], T.sc2[:, 15:287:16], A.subtract)
        op("V", ["pls", "kl17"], ["place"], vtt, c("place"), c("pls"), c("kl17"), A.add)

    def keep_keys():
        op("S", ["k2", "kapU"], ["Ko"], act, T.Ko[:], T.k2[:].indirect(c("kapU")), AF.Copy)

    def cells(n):
        op("V", ["place"], ["sh3"], vts, c("sh3"), c("place"), 3, None, A.arith_shift_right)
        op("V", ["sh3"], ["eqc"], vtt, c("eqc"), c("sh3", 0, 16), c("sh3", 1, 17), A.is_equal)
        op("V", ["eqc", "De"], ["dmc"], vtt, c("dmc"), c("eqc"), c("De"), A.mult)
        op("V", ["dmc", "sh3"], ["ofc"], vtt, c("ofc"), c("dmc"), c("sh3", 0, 16), A.max)
        op("V", ["ofc"], ["oc2"], vcp, c("oc2"), c("ofc"))
        op("V", ["oc2", "kvale"], ["Wc"], vcp, T.Wc[:].indirect(c("oc2")), T.kvale[:])
        op("V", ["Wc"], ["kpw"], vts, T.kpw[:], T.Wc[:, 0:256], 0.0, None, A.is_equal)
        op("V", ["Wc", "kpw"], ["Wr"], vscan, T.Wr[:], T.kpw[:], T.Wc[:, 0:256], 0.0, A.mult, A.add)
        if n < R - 1: zeros("Wc", 512, ["Wr"])
        op("V", ["Wr", "mask"], ["mkb"], vtt, T.mkb[:], T.Wr[:], T.mask[:], A.mult)
        op("V", ["mkb", "keepb"], ["mko"], vscan, T.mko[:], T.keepb[:], T.mkb[:], 0.0, A.mult, A.add)
        op("V", ["mko"], ["ku"], vts, c("ku"), T.mko[:, 15::16], -1.0, 0.0, A.add, A.max)

    XK = ["X0", "X1", "X2", "X3"]

    def tail():
        op("V", XK, ["Xt"], vcp, T.X[:, 1024:1084], T.X[:, 4:64])
        op("S", XK, ["Xu"], act, T.X[:, 1084:1088], T.X[:, 1020:1024], AF.Copy)
        op("V", XK + ["Xt", "Xu"], ["xq", "xs"], V.quantize_mx, T.xq[:], T.xs[:], T.X[:])

    def unpack_pairs():
        for t in range(4):
            mm("ps%d" % t, "ec%d" % t, "es%d" % t, 0, "xq", "xs", 0, 256, True, False)
            mm("ps%d" % t, "ec%d" % t, "es%d" % t, 0, "xq", "xs", 16, 256, False, True)
            op("S", ["ps%d" % t], ["P%d" % t], act, T.P[:, 256 * t:256 * t + 256], T["ps%d" % t][:, 0:256], AF.Copy)
        for t in range(4):
            mm("ps%d" % (4 + t), "ec%d" % t, "es%d" % t, 0, "xq", "xs", 0, 256)

    def unpack_keep():
        for t in range(4):
            op("S", ["ps%d" % (4 + t)], ["F%d" % t], act, T.F[:, 256 * t:256 * t + 256], T["ps%d" % (4 + t)][:, 0:256], AF.Copy, scale=2.0)

    def deal(t, key, out):
        op("V", ["H%d" % t, "hu", "G%d" % t], [key], vtt, out, T.H[:, 128 * t:128 * t + 128].indirect(c("hu")), T.G[:, 256 * t:256 * t + 256], A.add)

    order_begin(0)
    consts1()
    order_tables(0)
    for t in range(4):
        op("V", ["lo"], ["x4%d" % t], vts, c("x4%d" % t), c("lo"), 4.0, float(t), A.mult, A.add)
    for t in range(2):
        op("S", ["xin", "x4%d" % t], ["X%d" % t], act, T.X[:, t:1024:4], T.xin[:].indirect(c("x4%d" % t)), AF.Copy)
    for t in range(2, 4):
        op("V", ["xin", "x4%d" % t], ["X%d" % t], vcp, T.X[:, t:1024:4], T.xin[:].indirect(c("x4%d" % t)))
    tail()
    unpack_pairs()
    consts2()
    order_places()
    cells(0)
    quant("hc", "hs", "Bh", 0, 128)
    quant("mc", "ms", "Bm", 0, 128)
    keep_keys()
    dma("dw", [("Y", T.wq[:].bitcast(dt.uint8), T.wc[:], [], ["wq"]), ("Y", T.wp[:], T.ws[:], [], ["wp"])])
    dma("dv", [("Y", T.vin[:], T.v[:], [], ["vin"])])

    nxt = T.cores[(rank + 1) % N]
    rid, pid, sen = topo.addr(nxt)
    m4 = sum(1 << e for e in topo.engines(core, nxt)[0:4])

    for n in range(R):
        for t in (0, 1):
            op("V", ["P%d" % t, "ku"], ["Z%d" % t], vcp, T.Z[:, t:1024:4], T.P[:, 256 * t:256 * t + 256].indirect(c("ku")))
        for t in (2, 3):
            op("S", ["P%d" % t, "ku"], ["Z%d" % t], act, T.Z[:, t:1024:4], T.P[:, 256 * t:256 * t + 256].indirect(c("ku")), AF.Copy)
        op("V", ["Z0", "Z1", "Z2", "Z3"], ["zq", "zs"], V.quantize_mx, T.zq[:], T.zs[:], T.Z[:])
        mm("ps0", "u2", "u2s", 0, "zq", "zs", 0, 256)
        mm("ps1", "u2", "u2s", 0, "zq", "zs", 0, 256)
        op("V", ["sh3"], ["cu"], vcp, c("cu"), c("sh3", 0, 16))
        op("V", ["ps0", "mask"], ["mk2"], vtt, T.mk2[:], T.ps0[:, 0:256], T.mask[:], A.mult)
        op("V", ["mk2", "keepf"], ["sl"], vscan, T.sl[:], T.keepf[:], T.mk2[:], 0.0, A.mult, A.add)
        for j in range(NS):
            b = 16 - NS + j
            op("S", ["ps1", "sl"], ["sg%d" % j], act, T.sgn[:, 256 * j:256 * j + 256], T.ps1[:, 0:256], AF.Sign, bias=T.sl[:, 16 * b + 15:16 * b + 16], scale=-1.0)
            if j == 0:
                op("S", ["zs", "oddl"], ["pp%d" % n], act, T["pp%d" % n][:], T.zs[:].indirect(c("oddl", 0, 8)), AF.Copy)
                op("S", ["sl", "rep"], ["SBt"], act, T.SBt[:], T.sl[:].indirect(c("rep")), AF.Copy)
        for j in range(NS):
            b = 16 - NS + j
            o, ck, ce = 1024 * (b // 4) + b % 4, "S%d" % (b // 4), 1024 * (b // 4) + 1024
            op("S", ["sg%d" % j, "Ct"], [ck], act, T.Ct[:, o:o + 64 * b:4], T.sgn[:, 256 * j:256 * j + 16 * b], AF.Sign, bias=-0.5, scale=-1.0, acc=True)
            if b < 15: op("S", ["sg%d" % j, "Ct"], [ck], act, T.Ct[:, o + 64 * b + 64:ce:4], T.sgn[:, 256 * j + 16 * b + 16:256 * j + 256], AF.Sign, bias=0.5, scale=-1.0, acc=True)
        for b in range(16 - NS):
            k = b // 4
            o, s1 = 1024 * k + b % 4, T.sl[:, 16 * b + 15:16 * b + 16]
            if b: op("V", ["ps0", "sl", "Ct"], ["C%d" % k], vts, T.Ct[:, o:o + 64 * b:4], T.ps0[:, 0:16 * b], s1, None, A.is_gt, acc=True)
            op("V", ["ps0", "sl", "Ct"], ["C%d" % k], vts, T.Ct[:, o + 64 * b + 64:1024 * k + 1024:4], T.ps0[:, 16 * b + 16:256], s1, None, A.is_ge, acc=True)
            if b == 1:
                op("V", ["zq", "oddl"], ["pk%d" % n], vcp, T["pk%d" % n][:].bitcast(dt.uint32), T.zq[:].bitcast(dt.uint32).indirect(c("oddl", 0, 8)))
            if b == 7: op("V", ["C0", "C1", "Ct"], ["cq0"], V.quantize_mx, T.cq[:, 0:512], T.cs[:, 0:512], T.Ct[:, 0:2048])
        need("G", [last["pk%d" % n], last["pp%d" % n]])
        g.remote_dma(T["lc%d" % n][:].bitcast(dt.uint8), T["pk%d" % n][:].bitcast(dt.uint8), T.sem["arr%d" % n], T.sem.snd, pid, rid, m4)
        g.remote_dma(T["lp%d" % n][:], T["pp%d" % n][:], T.sem["arr%d" % n], T.sem.snd, pid, rid, m4)
        op("V", ["ps0", "SBt"], ["dd"], vtt, T.dd[:], T.ps0[:, 0:256], T.SBt[:], A.subtract)
        op("V", ["dd", "m0"], ["Dt"], vtt, T.Dt[:, 0::4], T.dd[:], T.m0[:], A.is_gt)
        op("V", ["C2", "S2", "Ct"] if NS < 8 else ["S2", "Ct"], ["cq2"], V.quantize_mx, T.cq[:, 512:768], T.cs[:, 512:768], T.Ct[:, 2048:3072])
        op("V", ["Dt"], ["dq"], V.quantize_mx, T.dq[:], T.dqs[:], T.Dt[:])
        op("V", ["S3", "Ct"], ["cq3"], V.quantize_mx, T.cq[:, 768:1024], T.cs[:, 768:1024], T.Ct[:, 3072:4096])

        def total(lq, ls, rq, rs, key, ra, start, stop):
            op("T", [lq, ls, key], ["ps2"], PE.matmul_mx, T.ps2[:, 0:256], T[lq][:], T[ls][:], T[rq][:, ra:ra + 256], T[rs][:, ra:ra + 256], start, stop, acc=not start)
        total("bc", "bs", "cq", "cs", "cq0", 0, True, False)
        total("bc", "bs", "cq", "cs", "cq0", 256, False, False)
        total("mc", "ms", "cq", "cs", "cq2", 512, False, False)
        total("bc", "bs", "dq", "dqs", "dq", 0, False, False)
        total("hc", "hs", "cq", "cs", "cq3", 768, False, True)
        op("V", ["ps2", "crow"], ["stw"], vtt, T.stw[:], T.ps2[:, 0:256], T.crow[:], A.add)
        op("V", ["stw", "cu", "mask"], ["mg"], vtt, T.mg[:], T.stw[:].indirect(c("cu")), T.mask[:], A.mult)
        op("V", ["stw", "cu", "Ko"], ["Krow"], vtt, T.Krow[:], T.stw[:].indirect(c("cu")), T.Ko[:], A.add)
        op("V", ["mg", "keepb"], ["mgo"], vscan, T.mgo[:], T.keepb[:], T.mg[:], 0.0, A.mult, A.add)
        op("V", ["mgo", "lk"], ["Kl"], vtt, c("Kl"), T.mgo[:, 15::16], c("lk", 0, 16), A.add)
        order_begin(n + 1)
        unpack_keep()
        if n == R - 1: quant("vq", "vqs", "vin", 0, 128)
        order_tables(n + 1)
        op("V", ["lo"], ["lou"], vcp, c("lou"), c("lo"))
        for t in range(4):
            op("S", ["F%d" % t, "lou"], ["G%d" % t], act, T.G[:, 256 * t:256 * t + 256], T.F[:, 256 * t:256 * t + 256].indirect(c("lou")), AF.Copy)
        need("T", [("arr%d" % n, 8, "R", {})])
        ends["arr%d" % n] = 8
        for t in range(4):
            mm("ps%d" % (4 + t), "wq", "wp", 128 * t, "lc%d" % n, "lp%d" % n, 0, 128)
            op("S", ["ps%d" % (4 + t)], ["H%d" % t], act, T.H[:, 128 * t:128 * t + 128], T["ps%d" % (4 + t)][:, 0:128], AF.Copy, scale=0.03125)
        keep_keys()
        if n == R - 1:
            op("G", [], ["ior"], g.iota, T.ior[:], [[1, 256]], 0, 0, allow_small_or_imprecise_dtypes=True)
            op("V", ["lk", "tt"], ["cf"], vtt, c("cf"), c("lk", 0, 16), c("tt", 0, 16), A.subtract)
            op("V", ["cf"], ["colI"], vts, c("colI"), c("cf"), 256.0, None, A.mult)
            op("V", ["colI"], ["c_lo"], vts, c("c_lo"), c("colI"), 15, None, A.bitwise_and)
            op("V", ["colI"], ["c_hi"], vts, c("c_hi"), c("colI"), 4, None, A.arith_shift_right)
            op("V", ["colI"], ["colU"], vcp, c("colU"), c("colI"))
            op("V", ["c_lo"], ["cf"], vts, c("cf"), c("c_lo"), 16.0, None, A.mult)
            op("V", ["cf", "c_hi"], ["cp"], vtt, c("cp"), c("cf"), c("c_hi"), A.add)
            op("V", ["cp"], ["piU"], vcp, c("piU"), c("cp"))
            op("V", ["piU", "ior"], ["inv"], vcp, T.inv[:].indirect(c("piU")), T.ior[:])
            dma("div", [("Y", c("ivl"), T.inv[0::16, :], ["inv"], ["ivl"])])
        order_places()
        op("V", ["place"], ["sh4"], vts, c("sh4"), c("place", 0, 16), 4, None, A.arith_shift_right)
        op("V", ["sh4"], ["hu"], vcp, c("hu"), c("sh4"))
        if n < R - 1:
            for t in range(4): deal(t, "X%d" % t, T.X[:, t:1024:4])
            tail()
            unpack_pairs()
            cells(n + 1)
        else:
            op("V", ["ivl"], ["iu"], vcp, c("iu"), c("ivl"))
            for t in range(4):
                deal(t, "XP%d" % t, T.XP[:, 256 * t:256 * t + 256])
                if t < 3: op("S", ["XP%d" % t, "iu"], ["Xf%d" % t], act, T.Xf[:, t:1024:4], T.XP[:, 256 * t:256 * t + 256].indirect(c("iu")), AF.Copy)
                else: op("V", ["XP%d" % t, "iu"], ["Xf%d" % t], vcp, T.Xf[:, t:1024:4], T.XP[:, 256 * t:256 * t + 256].indirect(c("iu")))

    op("V", ["Xf0", "Xf1", "Xf2", "Xf3"], ["fq", "fqs"], V.quantize_mx, T.fq[:], T.fqs[:], T.Xf[:])
    mm("ps0", "vq", "vqs", 0, "fq", "fqs", 0, 256)
    op("V", ["Ko", "colU"], ["prs"], vcp, T.prs[:].indirect(c("colU")), T.Ko[:])
    dma("dend", [("Y", T.oc[:], T.fq[:].bitcast(dt.uint8), ["fq"], [])] + [("YS"[k % 2], T.osc[4 * k:4 * k + 4, :], T.fqs[32 * k:32 * k + 4, :], ["fqs"], []) for k in range(4)])
    op("S", ["ps0"], ["yo"], act, T.yo[:], T.ps0[:, 0:256], AF.Copy)
    op("V", ["prs"], ["pti"], vts, T.pti[:], T.prs[:], -0.498, None, A.add)
    op("V", ["pti"], ["ptf"], vcp, T.ptf[:], T.pti[:])
    dma("dend", [("S", T.y[:], T.yo[:], ["yo"], []), ("Y", T.pt[:], T.ptf[0::16, :], ["ptf"], [])])
    for s, v in ends.items(): g.wait_ge(T.sem[s], v)
    g.wait_ge(T.sem.snd, 8 * R)
